import numpy as np
import ml_dtypes


def mxq(x, axis, fmt="e4m3"):
    dtype, down = {"e4m3": (ml_dtypes.float8_e4m3fn, 7), "e5m2": (ml_dtypes.float8_e5m2, 14)}[fmt]
    v = np.moveaxis(np.asarray(x, np.float32).astype(ml_dtypes.bfloat16).astype(np.float64), axis, -1)
    blocks = v.reshape(v.shape[:-1] + (-1, 32))
    amax = np.abs(blocks).max(-1, keepdims=True)
    byte = np.maximum(np.where(amax > 0, np.frexp(amax)[1] - 1 + 127, 0) - down, 1)
    scale = np.exp2(byte - 127.0)
    codes = (blocks / scale).astype(np.float32).astype(dtype).astype(np.float64)
    return np.moveaxis((codes * scale).reshape(v.shape), -1, axis)


WIDE = False


def mx_kscale(k):
    if not WIDE:
        return np.ones(k)
    levels = np.array([10, -10, 5, -5, 0])
    if k % 512:
        return np.exp2(np.random.permutation(np.resize(levels, k // 32))).repeat(32)
    a = np.empty((k // 512, 16))
    for p in range(k // 512):
        a[p, :8] = np.random.permutation(np.resize(levels, 8))
        for g in range(8):
            far = levels[np.abs(levels - a[p, g]) >= 10]
            a[p, g + 8] = far[np.random.randint(len(far))]
    return np.exp2(a.ravel()).repeat(32)


def f64(x):
    return np.asarray(x).astype(np.float64)


def striped(idx):
    return np.tile(idx.reshape(-1, 16).T, (8, 1)).astype(np.uint16)


def unstriped(offs):
    return offs[:16].T.reshape(-1).astype(np.int64)


def pack_weight(w):
    k, n = w.shape
    w = f64(np.asarray(w, np.float32).astype(ml_dtypes.bfloat16)).reshape(k // 32, 32, n)
    amax = np.abs(w).max(1)
    byte = np.clip(np.where(amax > 0, np.frexp(amax)[1] - 1 + 127 - 7, 1), 1, 254)
    scaled = (w * np.exp2(127.0 - byte)[:, None, :]).reshape(k, n).astype(np.float32)
    words = np.ascontiguousarray(scaled.reshape(k // 512, 128, 4, n).transpose(0, 1, 3, 2)).astype(ml_dtypes.float8_e4m3fn).view(np.uint8)
    return words, np.ascontiguousarray(byte.astype(np.uint8).reshape(k // 512, 16, n))


def unpack_weight(words, scales):
    g, p, n, _ = words.shape
    vals = np.ascontiguousarray(words).view(ml_dtypes.float8_e4m3fn).astype(np.float64) * np.repeat(np.exp2(scales.astype(np.float64) - 127.0), 8, axis=1)[..., None]
    return vals.transpose(0, 1, 3, 2).reshape(g * 512, n)


K, T, S, N = 512, 2048, 1024, 128


def setup_inputs():
    n = np.random.standard_normal
    s = mx_kscale(K)[:, None]
    packed_xT = pack_weight(n((K, T)) * s)
    return {
        "x_words": packed_xT[0],
        "x_scales": packed_xT[1],
        "w1": (n((K, N)) / np.sqrt(K) / s).astype(np.float32),
        "w2": (n((K, N)) / np.sqrt(K) / s).astype(np.float32),
        "ker1": (np.random.uniform(0.5, 0.8, (N, 1))).astype(np.float32),
        "ker2": (np.random.uniform(0.3, 0.6, (N, 1))).astype(np.float32),
        "ker3": (np.random.uniform(0.1, 0.4, (N, 1))).astype(np.float32),
        "offs": striped(np.random.permutation(T)[:S]),
    }


def reference(x_words, x_scales, w1, w2, ker1, ker2, ker3, offs):
    xq = unpack_weight(x_words, x_scales)[:, unstriped(offs)]
    ys = mxq(f64(w2), 0, "e4m3").T @ xq
    yv = mxq(f64(w1), 0, "e4m3").T @ xq
    imp = (ys * (np.sqrt(np.log(np.exp(yv) + 1.0)))) / (np.abs(ys) + 0.3)
    move = imp + f64(ker1) * (np.pad(imp, ((0, 0), (1, 0)))[:, :S]) + f64(ker2) * (np.pad(imp, ((0, 0), (2, 0)))[:, :S]) + f64(ker3) * (np.pad(imp, ((0, 0), (3, 0)))[:, :S])
    return move * ys

@@ -1,0 +1,192 @@
+from contextlib import ExitStack
+
+import concourse.mybir as mybir
+
+K, T, S, M = 512, 2048, 1024, 128
+FLOPS = 2 * 2 * K * M * S
+
+F32 = mybir.dt.float32
+BF16 = mybir.dt.bfloat16
+I32 = mybir.dt.int32
+U32 = mybir.dt.uint32
+U16 = mybir.dt.uint16
+U8 = mybir.dt.uint8
+FP8X4 = mybir.dt.float8_e4m3fn_x4
+ALU = mybir.AluOpType
+ACT = mybir.ActivationFunctionType
+
+P = 128
+PACK = 4
+BANK = 512
+PIECE = 256
+PAD = 4
+SOFT = 0.3
+EXP_CAP = 2.0 ** 60
+TINY = 1e-30
+
+
+def tile_picked_yimpct_cost_p_kernel(
+    tc, x_words, x_scales, w1, w2, ker1, ker2, ker3, offs, out
+):
+    nc = tc.nc
+    with ExitStack() as ctx:
+        sb = ctx.enter_context(tc.tile_pool(name="sb", bufs=1))
+        ps = ctx.enter_context(tc.psum_pool(name="ps", bufs=1))
+
+        offsets = sb.tile([P, S // 16], U16, name="offsets")
+        nc.sync.dma_start(offsets[:], offs)
+
+        scale_table = sb.tile([P, T], U8, name="scale_table", align_bytes=64)
+        nc.vector.memset(scale_table[:].bitcast(I32), 0)
+        w1_raw = sb.tile([P, PACK, M], F32, name="w1_raw")
+        nc.sync.dma_start(out=w1_raw[:], in_=w1.rearrange("(p j) m -> p j m", j=PACK))
+        for q, queue in enumerate((nc.sync, nc.scalar, nc.sync, nc.scalar)):
+            queue.dma_start(
+                out=scale_table[32 * q : 32 * q + 4, :].bitcast(I32),
+                in_=x_scales[0, 4 * q : 4 * q + 4, :].bitcast(I32),
+            )
+        word_table = sb.tile([P, T], I32, name="word_table", align_bytes=64)
+        nc.sync.dma_start(out=word_table[:], in_=x_words[0].rearrange("p c r -> p (c r)").bitcast(I32))
+        w2_raw = sb.tile([P, PACK, M], F32, name="w2_raw")
+        nc.sync.dma_start(out=w2_raw[:], in_=w2.rearrange("(p j) m -> p j m", j=PACK))
+
+        kers = []
+        for i, ker in enumerate((ker1, ker2, ker3)):
+            col = sb.tile([P, 1], F32, name="ker%d" % (i + 1))
+            nc.gpsimd.dma_start(out=col[:], in_=ker)
+            kers.append(col)
+
+        imp = sb.tile([P, PAD + S], F32, name="imp")
+        nc.vector.memset(imp[:, 1:PAD], 0.0)
+
+        def round_weight(raw, name):
+            grouped = sb.tile([P, M, PACK], BF16, name=name + "_bf16", align_bytes=64)
+            nc.scalar.activation(out=grouped[:], in_=raw[:].rearrange("p j m -> p m j"), func=ACT.Copy)
+            return grouped
+
+        def quantize_weight(grouped, name):
+            codes = sb.tile([P, M], U32, name=name + "_codes", align_bytes=64)
+            scales = sb.tile([P, M], U8, name=name + "_scales", align_bytes=64)
+            nc.vector.quantize_mx(
+                out=codes[:].bitcast(FP8X4), scales=scales[:], in_=grouped[:].rearrange("p m j -> p (m j)")
+            )
+            return codes, scales
+
+        x_codes = sb.tile([P, S], U32, name="x_codes", align_bytes=64)
+        x_bytes = sb.tile([P, S], U8, name="x_bytes", align_bytes=64)
+        nc.vector.tensor_copy(out=x_bytes[:], in_=scale_table[:].indirect(offsets[:]))
+
+        w1_q = quantize_weight(round_weight(w1_raw, "w1"), "w1")
+        w2_bf16 = round_weight(w2_raw, "w2")
+
+        yv = [ps.tile([P, BANK], F32, name="yv%d" % h) for h in range(2)]
+        ys = [ps.tile([P, BANK], F32, name="ys%d" % h) for h in range(2)]
+        e = sb.tile([P, S], F32, name="e")
+        a = sb.tile([P, S], F32, name="a")
+
+        def product(banks, weight, c0):
+            cols = slice(c0, c0 + PIECE)
+            target = banks[c0 // BANK][:, c0 % BANK : c0 % BANK + PIECE]
+            nc.tensor.matmul_mx(
+                out=target,
+                lhsT=weight[0][:].bitcast(FP8X4),
+                lhsT_scale=weight[1][:],
+                rhs=x_codes[:, cols].bitcast(FP8X4),
+                rhs_scale=x_bytes[:, cols],
+                start=True,
+                stop=True,
+            )
+            return target
+
+        w2_q = None
+        order = [0, 2 * PIECE, PIECE, 3 * PIECE]
+        for n, c0 in enumerate(order):
+            nc.vector.tensor_copy(
+                out=x_codes[:, c0 : c0 + PIECE],
+                in_=word_table[:].bitcast(U32).indirect(offsets[:, c0 // 16 : (c0 + PIECE) // 16]),
+            )
+            nc.scalar.activation(out=e[:, c0 : c0 + PIECE], in_=product(yv, w1_q, c0), func=ACT.Exp)
+            if n == 1:
+                w2_q = quantize_weight(w2_bf16, "w2")
+            if n >= 1:
+                p0 = order[n - 1]
+                nc.scalar.activation(out=a[:, p0 : p0 + PIECE], in_=product(ys, w2_q, p0), func=ACT.Abs)
+        p0 = order[-1]
+        last_ys = product(ys, w2_q, p0)
+
+        ec = sb.tile([P, S], F32, name="ec")
+        nc.vector.tensor_scalar(out=ec[:], in0=e[:], scalar1=EXP_CAP, scalar2=None, op0=ALU.min)
+
+        neg = sb.tile([P, PIECE], F32, name="neg")
+        nc.vector.tensor_scalar(out=neg[:], in0=last_ys, scalar1=-1.0, scalar2=None, op0=ALU.mult)
+        nc.vector.tensor_tensor(out=a[:, p0 : p0 + PIECE], in0=last_ys, in1=neg[:], op=ALU.max)
+
+        halves = [slice(h * BANK, (h + 1) * BANK) for h in range(2)]
+        lg = sb.tile([P, S], F32, name="lg")
+        for cols in halves:
+            nc.scalar.activation(out=lg[:, cols], in_=ec[:, cols], func=ACT.Ln, bias=1.0)
+
+        poly = sb.tile([P, S], F32, name="poly")
+        sp = sb.tile([P, S], F32, name="sp")
+        q = sb.tile([P, S], F32, name="q")
+        num = sb.tile([P, S], F32, name="num")
+        r = sb.tile([P, S], F32, name="r")
+        acc1 = sb.tile([P, S], F32, name="acc1")
+        acc2 = sb.tile([P, S], F32, name="acc2")
+        move = sb.tile([P, S], F32, name="move")
+        res = sb.tile([P, S], F32, name="res")
+
+        def stt(o, i0, s, i1, op0, op1):
+            nc.vector.scalar_tensor_tensor(out=o, in0=i0, scalar=s, in1=i1, op0=op0, op1=op1)
+
+        for h, cols in enumerate(halves):
+            stt(poly[:, cols], a[:, cols], 2 * SOFT, a[:, cols], ALU.add, ALU.mult)
+        def volume(h):
+            stt(sp[:, halves[h]], yv[h][:], TINY, lg[:, halves[h]], ALU.max, ALU.max)
+
+        def radicand(h):
+            cols = halves[h]
+            stt(q[:, cols], poly[:, cols], SOFT * SOFT, sp[:, cols], ALU.add, ALU.mult)
+            nc.scalar.activation(out=r[:, cols], in_=q[:, cols], func=ACT.Abs_reciprocal_sqrt)
+
+        def numerator(h):
+            nc.vector.tensor_tensor(out=num[:, halves[h]], in0=ys[h][:], in1=sp[:, halves[h]], op=ALU.mult)
+
+        def shifted(cols, by):
+            return imp[:, PAD + cols.start - by : PAD + cols.stop - by]
+
+        def impact(h):
+            cols = halves[h]
+            nc.vector.tensor_tensor(out=shifted(cols, 0), in0=num[:, cols], in1=r[:, cols], op=ALU.mult)
+
+        sums = [None, acc1, acc2, move]
+
+        def tap(i, h):
+            cols = halves[h]
+            before = shifted(cols, 0) if i == 1 else sums[i - 1][:, cols]
+            stt(sums[i][:, cols], shifted(cols, i), kers[i - 1][:], before, ALU.mult, ALU.add)
+
+        def cost(c0):
+            cols = slice(c0, c0 + PIECE)
+            signed = ys[c0 // BANK][:, c0 % BANK : c0 % BANK + PIECE]
+            nc.vector.tensor_tensor(out=res[:, cols], in0=signed, in1=move[:, cols], op=ALU.mult)
+            nc.sync.dma_start(out=out[:, cols], in_=res[:, cols])
+
+        volume(0)
+        volume(1)
+        radicand(0)
+        radicand(1)
+        numerator(0)
+        impact(0)
+        numerator(1)
+        tap(1, 0)
+        impact(1)
+        tap(2, 0)
+        tap(1, 1)
+        tap(3, 0)
+        tap(2, 1)
+        cost(0)
+        tap(3, 1)
+        cost(PIECE)
+        cost(2 * PIECE)
+        cost(3 * PIECE)

@@ -45,39 +45,37 @@ def tile_picked_yimpct_cost_p_kernel(
                 out=scale_table[32 * q : 32 * q + 4, :].bitcast(I32),
                 in_=x_scales[0, 4 * q : 4 * q + 4, :].bitcast(I32),
             )
-        word_table = sb.tile([P, T], I32, name="word_table", align_bytes=64)
-        nc.sync.dma_start(out=word_table[:], in_=x_words[0].rearrange("p c r -> p (c r)").bitcast(I32))
         w2_raw = sb.tile([P, PACK, M], F32, name="w2_raw")
         nc.sync.dma_start(out=w2_raw[:], in_=w2.rearrange("(p j) m -> p j m", j=PACK))
+        word_table = sb.tile([P, T], I32, name="word_table", align_bytes=64)
+        nc.sync.dma_start(out=word_table[:], in_=x_words[0].rearrange("p c r -> p (c r)").bitcast(I32))
 
         kers = []
         for i, ker in enumerate((ker1, ker2, ker3)):
             col = sb.tile([P, 1], F32, name="ker%d" % (i + 1))
-            nc.gpsimd.dma_start(out=col[:], in_=ker)
+            nc.sync.dma_start(out=col[:], in_=ker)
             kers.append(col)
 
         imp = sb.tile([P, PAD + S], F32, name="imp")
         nc.vector.memset(imp[:, 1:PAD], 0.0)
 
-        def round_weight(raw, name):
-            grouped = sb.tile([P, M, PACK], BF16, name=name + "_bf16", align_bytes=64)
-            nc.scalar.activation(out=grouped[:], in_=raw[:].rearrange("p j m -> p m j"), func=ACT.Copy)
-            return grouped
-
-        def quantize_weight(grouped, name):
-            codes = sb.tile([P, M], U32, name=name + "_codes", align_bytes=64)
-            scales = sb.tile([P, M], U8, name=name + "_scales", align_bytes=64)
-            nc.vector.quantize_mx(
-                out=codes[:].bitcast(FP8X4), scales=scales[:], in_=grouped[:].rearrange("p m j -> p (m j)")
+        grouped = sb.tile([P, 2 * M * PACK], BF16, name="w_bf16", align_bytes=64)
+        for i, raw in enumerate((w1_raw, w2_raw)):
+            nc.scalar.activation(
+                out=grouped[:, i * M * PACK : (i + 1) * M * PACK].rearrange("p (m j) -> p m j", j=PACK),
+                in_=raw[:].rearrange("p j m -> p m j"),
+                func=ACT.Copy,
             )
-            return codes, scales
 
         x_codes = sb.tile([P, S], U32, name="x_codes", align_bytes=64)
         x_bytes = sb.tile([P, S], U8, name="x_bytes", align_bytes=64)
         nc.vector.tensor_copy(out=x_bytes[:], in_=scale_table[:].indirect(offsets[:]))
 
-        w1_q = quantize_weight(round_weight(w1_raw, "w1"), "w1")
-        w2_bf16 = round_weight(w2_raw, "w2")
+        w_codes = sb.tile([P, 2 * M], U32, name="w_codes", align_bytes=64)
+        w_bytes = sb.tile([P, 2 * M], U8, name="w_bytes", align_bytes=64)
+        nc.vector.quantize_mx(out=w_codes[:].bitcast(FP8X4), scales=w_bytes[:], in_=grouped[:])
+        w1_q = (w_codes[:, 0:M], w_bytes[:, 0:M])
+        w2_q = (w_codes[:, M : 2 * M], w_bytes[:, M : 2 * M])
 
         yv = [ps.tile([P, BANK], F32, name="yv%d" % h) for h in range(2)]
         ys = [ps.tile([P, BANK], F32, name="ys%d" % h) for h in range(2)]
@@ -89,8 +87,8 @@ def tile_picked_yimpct_cost_p_kernel(
             target = banks[c0 // BANK][:, c0 % BANK : c0 % BANK + PIECE]
             nc.tensor.matmul_mx(
                 out=target,
-                lhsT=weight[0][:].bitcast(FP8X4),
-                lhsT_scale=weight[1][:],
+                lhsT=weight[0].bitcast(FP8X4),
+                lhsT_scale=weight[1],
                 rhs=x_codes[:, cols].bitcast(FP8X4),
                 rhs_scale=x_bytes[:, cols],
                 start=True,
@@ -98,7 +96,6 @@ def tile_picked_yimpct_cost_p_kernel(
             )
             return target
 
-        w2_q = None
         order = [0, 2 * PIECE, PIECE, 3 * PIECE]
         for n, c0 in enumerate(order):
             nc.vector.tensor_copy(
@@ -106,24 +103,23 @@ def tile_picked_yimpct_cost_p_kernel(
                 in_=word_table[:].bitcast(U32).indirect(offsets[:, c0 // 16 : (c0 + PIECE) // 16]),
             )
             nc.scalar.activation(out=e[:, c0 : c0 + PIECE], in_=product(yv, w1_q, c0), func=ACT.Exp)
-            if n == 1:
-                w2_q = quantize_weight(w2_bf16, "w2")
-            if n >= 1:
-                p0 = order[n - 1]
-                nc.scalar.activation(out=a[:, p0 : p0 + PIECE], in_=product(ys, w2_q, p0), func=ACT.Abs)
-        p0 = order[-1]
-        last_ys = product(ys, w2_q, p0)
+            if n < 2:
+                nc.scalar.activation(out=a[:, c0 : c0 + PIECE], in_=product(ys, w2_q, c0), func=ACT.Abs)
 
         ec = sb.tile([P, S], F32, name="ec")
         nc.vector.tensor_scalar(out=ec[:], in0=e[:], scalar1=EXP_CAP, scalar2=None, op0=ALU.min)
 
-        neg = sb.tile([P, PIECE], F32, name="neg")
-        nc.vector.tensor_scalar(out=neg[:], in0=last_ys, scalar1=-1.0, scalar2=None, op0=ALU.mult)
-        nc.vector.tensor_tensor(out=a[:, p0 : p0 + PIECE], in0=last_ys, in1=neg[:], op=ALU.max)
+        neg = sb.tile([P, 2, PIECE], F32, name="neg")
+        late = [product(ys, w2_q, c0) for c0 in order[2:]]
+        for n, signed in enumerate(late):
+            nc.vector.tensor_scalar(out=neg[:, n, :], in0=signed, scalar1=-1.0, scalar2=None, op0=ALU.mult)
+        for n, signed in enumerate(late):
+            c0 = order[2 + n]
+            nc.vector.tensor_tensor(out=a[:, c0 : c0 + PIECE], in0=signed, in1=neg[:, n, :], op=ALU.max)
 
         halves = [slice(h * BANK, (h + 1) * BANK) for h in range(2)]
         lg = sb.tile([P, S], F32, name="lg")
-        for cols in halves:
+        for cols in (slice(0, PIECE), slice(PIECE, S)):
             nc.scalar.activation(out=lg[:, cols], in_=ec[:, cols], func=ACT.Ln, bias=1.0)
 
         poly = sb.tile([P, S], F32, name="poly")
@@ -141,8 +137,9 @@ def tile_picked_yimpct_cost_p_kernel(
 
         for h, cols in enumerate(halves):
             stt(poly[:, cols], a[:, cols], 2 * SOFT, a[:, cols], ALU.add, ALU.mult)
-        def volume(h):
-            stt(sp[:, halves[h]], yv[h][:], TINY, lg[:, halves[h]], ALU.max, ALU.max)
+        def volume(c0, n):
+            bank = yv[c0 // BANK][:, c0 % BANK : c0 % BANK + n]
+            stt(sp[:, c0 : c0 + n], bank, TINY, lg[:, c0 : c0 + n], ALU.max, ALU.max)
 
         def radicand(h):
             cols = halves[h]
@@ -172,8 +169,9 @@ def tile_picked_yimpct_cost_p_kernel(
             nc.vector.tensor_tensor(out=res[:, cols], in0=signed, in1=move[:, cols], op=ALU.mult)
             nc.sync.dma_start(out=out[:, cols], in_=res[:, cols])
 
-        volume(0)
-        volume(1)
+        volume(0, PIECE)
+        volume(PIECE, PIECE)
+        volume(BANK, BANK)
         radicand(0)
         radicand(1)
         numerator(0)

@@ -1,6 +1,7 @@
 from contextlib import ExitStack
 
 import concourse.mybir as mybir
+from concourse.masks import make_identity
 
 K, T, S, M = 512, 2048, 1024, 128
 FLOPS = 2 * 2 * K * M * S
@@ -20,6 +21,8 @@ PACK = 4
 BANK = 512
 PIECE = 256
 PAD = 4
+BLOCKS = 3
+HEAD = BLOCKS * P
 SOFT = 0.3
 EXP_CAP = 2.0 ** 60
 TINY = 1e-30
@@ -58,6 +61,9 @@ def tile_picked_yimpct_cost_p_kernel(
 
         imp = sb.tile([P, PAD + S], F32, name="imp")
         nc.vector.memset(imp[:, 1:PAD], 0.0)
+        ident = sb.tile([P, P], F32, name="ident")
+        nc.vector.memset(ident[:], 0.0)
+        make_identity(nc, ident[:], nomemset=True)
 
         grouped = sb.tile([P, 2 * M * PACK], BF16, name="w_bf16", align_bytes=64)
         for i, raw in enumerate((w1_raw, w2_raw)):
@@ -106,27 +112,46 @@ def tile_picked_yimpct_cost_p_kernel(
             if n < 2:
                 nc.scalar.activation(out=a[:, c0 : c0 + PIECE], in_=product(ys, w2_q, c0), func=ACT.Abs)
 
-        ec = sb.tile([P, S], F32, name="ec")
-        nc.vector.tensor_scalar(out=ec[:], in0=e[:], scalar1=EXP_CAP, scalar2=None, op0=ALU.min)
+        poly = sb.tile([P, S], F32, name="poly")
 
-        neg = sb.tile([P, 2, PIECE], F32, name="neg")
+        def by_arrival(tile, late):
+            return tile[:].rearrange("p (h l c) -> p l h c", h=2, l=2)[:, late]
+
+        d = sb.tile([P, S], F32, name="d")
+
+        def square(late):
+            nc.vector.tensor_tensor(
+                out=by_arrival(poly, late), in0=by_arrival(d, late), in1=by_arrival(d, late), op=ALU.mult
+            )
+
+        nc.vector.tensor_scalar(out=by_arrival(d, 0), in0=by_arrival(a, 0), scalar1=SOFT, scalar2=None, op0=ALU.add)
+        square(0)
+        ec = sb.tile([P, S], F32, name="ec")
+        nc.gpsimd.tensor_scalar(out=ec[:], in0=e[:], scalar1=EXP_CAP, scalar2=0.0, op0=ALU.min, op1=ALU.max)
+
+        neg_tile = sb.tile([P, BANK], F32, name="neg")
+        neg = [neg_tile[:, 0:PIECE], neg_tile[:, PIECE:BANK]]
         late = [product(ys, w2_q, c0) for c0 in order[2:]]
         for n, signed in enumerate(late):
-            nc.vector.tensor_scalar(out=neg[:, n, :], in0=signed, scalar1=-1.0, scalar2=None, op0=ALU.mult)
+            nc.vector.tensor_scalar(out=neg[n], in0=signed, scalar1=-1.0, scalar2=SOFT, op0=ALU.mult, op1=ALU.add)
         for n, signed in enumerate(late):
             c0 = order[2 + n]
-            nc.vector.tensor_tensor(out=a[:, c0 : c0 + PIECE], in0=signed, in1=neg[:, n, :], op=ALU.max)
+            nc.vector.scalar_tensor_tensor(
+                out=d[:, c0 : c0 + PIECE], in0=signed, scalar=SOFT, in1=neg[n], op0=ALU.add, op1=ALU.max
+            )
+        square(1)
 
         halves = [slice(h * BANK, (h + 1) * BANK) for h in range(2)]
-        lg = sb.tile([P, S], F32, name="lg")
-        for cols in (slice(0, PIECE), slice(PIECE, S)):
-            nc.scalar.activation(out=lg[:, cols], in_=ec[:, cols], func=ACT.Ln, bias=1.0)
+        lg_tile = sb.tile([P, S], F32, name="lg")
+        lg = [lg_tile[:, 0:PIECE], lg_tile[:, PIECE:BANK], lg_tile[:, BANK:S]]
+        for n, cols in enumerate((slice(0, PIECE), slice(PIECE, BANK), halves[1])):
+            nc.scalar.activation(out=lg[n], in_=ec[:, cols], func=ACT.Ln, bias=1.0)
 
-        poly = sb.tile([P, S], F32, name="poly")
         sp = sb.tile([P, S], F32, name="sp")
         q = sb.tile([P, S], F32, name="q")
-        num = sb.tile([P, S], F32, name="num")
+        num_tile = sb.tile([P, S], F32, name="num")
         r = sb.tile([P, S], F32, name="r")
+        num = [num_tile[:, cols] for cols in halves]
         acc1 = sb.tile([P, S], F32, name="acc1")
         acc2 = sb.tile([P, S], F32, name="acc2")
         move = sb.tile([P, S], F32, name="move")
@@ -135,56 +160,77 @@ def tile_picked_yimpct_cost_p_kernel(
         def stt(o, i0, s, i1, op0, op1):
             nc.vector.scalar_tensor_tensor(out=o, in0=i0, scalar=s, in1=i1, op0=op0, op1=op1)
 
-        for h, cols in enumerate(halves):
-            stt(poly[:, cols], a[:, cols], 2 * SOFT, a[:, cols], ALU.add, ALU.mult)
-        def volume(c0, n):
+        def volume(c0, n, log):
             bank = yv[c0 // BANK][:, c0 % BANK : c0 % BANK + n]
-            stt(sp[:, c0 : c0 + n], bank, TINY, lg[:, c0 : c0 + n], ALU.max, ALU.max)
+            stt(sp[:, c0 : c0 + n], bank, TINY, log, ALU.max, ALU.max)
 
         def radicand(h):
             cols = halves[h]
-            stt(q[:, cols], poly[:, cols], SOFT * SOFT, sp[:, cols], ALU.add, ALU.mult)
+            engine = nc.vector if h == 0 else nc.gpsimd
+            engine.tensor_tensor(out=q[:, cols], in0=poly[:, cols], in1=sp[:, cols], op=ALU.mult)
             nc.scalar.activation(out=r[:, cols], in_=q[:, cols], func=ACT.Abs_reciprocal_sqrt)
 
         def numerator(h):
-            nc.vector.tensor_tensor(out=num[:, halves[h]], in0=ys[h][:], in1=sp[:, halves[h]], op=ALU.mult)
+            nc.vector.tensor_tensor(out=num[h], in0=ys[h][:], in1=sp[:, halves[h]], op=ALU.mult)
 
         def shifted(cols, by):
             return imp[:, PAD + cols.start - by : PAD + cols.stop - by]
 
         def impact(h):
             cols = halves[h]
-            nc.vector.tensor_tensor(out=shifted(cols, 0), in0=num[:, cols], in1=r[:, cols], op=ALU.mult)
+            nc.vector.tensor_tensor(out=shifted(cols, 0), in0=num[h], in1=r[:, cols], op=ALU.mult)
 
         sums = [None, acc1, acc2, move]
 
-        def tap(i, h):
-            cols = halves[h]
+        def tap(i, cols):
             before = shifted(cols, 0) if i == 1 else sums[i - 1][:, cols]
             stt(sums[i][:, cols], shifted(cols, i), kers[i - 1][:], before, ALU.mult, ALU.add)
 
-        def cost(c0):
-            cols = slice(c0, c0 + PIECE)
-            signed = ys[c0 // BANK][:, c0 % BANK : c0 % BANK + PIECE]
-            nc.vector.tensor_tensor(out=res[:, cols], in0=signed, in1=move[:, cols], op=ALU.mult)
+        def cost(cols):
+            cut = min(max(BANK, cols.start), cols.stop)
+            for c0, c1 in ((cols.start, cut), (cut, cols.stop)):
+                if c1 > c0:
+                    signed = ys[c0 // BANK][:, c0 % BANK : c0 % BANK + c1 - c0]
+                    nc.vector.tensor_tensor(out=res[:, c0:c1], in0=signed, in1=move[:, c0:c1], op=ALU.mult)
             nc.sync.dma_start(out=out[:, cols], in_=res[:, cols])
 
-        volume(0, PIECE)
-        volume(PIECE, PIECE)
-        volume(BANK, BANK)
+        volume(0, PIECE, lg[0])
+        volume(PIECE, PIECE, lg[1])
+        volume(BANK, BANK, lg[2])
         radicand(0)
-        radicand(1)
         numerator(0)
+        radicand(1)
         impact(0)
+        head = slice(0, HEAD)
+        ys_head = q[:, head]
+        nc.scalar.activation(out=ys_head, in_=ys[0][:, head], func=ACT.Copy)
         numerator(1)
-        tap(1, 0)
         impact(1)
-        tap(2, 0)
-        tap(1, 1)
-        tap(3, 0)
-        tap(2, 1)
-        cost(0)
-        tap(3, 1)
-        cost(PIECE)
-        cost(2 * PIECE)
-        cost(3 * PIECE)
+
+        turned = [ps.tile([P, P], F32, name="turned%d" % b) for b in range(BLOCKS)]
+        scaled = sb.tile([P, 3, HEAD], F32, name="scaled")
+        for i in range(4):
+            if i == 0:
+                term = shifted(head, 0)
+            else:
+                term = scaled[:, i - 1, :]
+                nc.scalar.activation(out=term, in_=shifted(head, i), func=ACT.Copy, scale=kers[i - 1][:])
+            for b in range(BLOCKS):
+                nc.tensor.matmul(
+                    turned[b][:], term[:, b * P : (b + 1) * P], ident[:], start=(i == 0), stop=(i == 3), is_transpose=True
+                )
+        turned_sb = sb.tile([P, HEAD], F32, name="turned_sb")
+        move_head = ps.tile([P, HEAD], F32, name="move_head")
+        for b in range(BLOCKS):
+            nc.scalar.copy(out=turned_sb[:, b * P : (b + 1) * P], in_=turned[b][:])
+            nc.tensor.transpose(move_head[:, b * P : (b + 1) * P], turned_sb[:, b * P : (b + 1) * P], ident[:])
+
+        mid = (HEAD + S) // 2
+        streams = (slice(HEAD, mid), slice(mid, S))
+        for i in (1, 2, 3):
+            for cols in streams:
+                tap(i, cols)
+        for cols in streams:
+            cost(cols)
+        nc.vector.tensor_tensor(out=res[:, head], in0=move_head[:], in1=ys_head, op=ALU.mult)
+        nc.sync.dma_start(out=out[:, head], in_=res[:, head])

@@ -21,7 +21,7 @@ PACK = 4
 BANK = 512
 PIECE = 256
 PAD = 4
-BLOCKS = 3
+BLOCKS = 4
 HEAD = BLOCKS * P
 SOFT = 0.3
 EXP_CAP = 2.0 ** 60
@@ -83,7 +83,7 @@ def tile_picked_yimpct_cost_p_kernel(
         w1_q = (w_codes[:, 0:M], w_bytes[:, 0:M])
         w2_q = (w_codes[:, M : 2 * M], w_bytes[:, M : 2 * M])
 
-        yv = [ps.tile([P, BANK], F32, name="yv%d" % h) for h in range(2)]
+        yv = [ps.tile([P, BANK], F32, name="yv%d" % h, tag="bank%d" % h) for h in range(2)]
         ys = [ps.tile([P, BANK], F32, name="ys%d" % h) for h in range(2)]
         e = sb.tile([P, S], F32, name="e")
         a = sb.tile([P, S], F32, name="a")
@@ -202,12 +202,10 @@ def tile_picked_yimpct_cost_p_kernel(
         radicand(1)
         impact(0)
         head = slice(0, HEAD)
-        ys_head = q[:, head]
-        nc.scalar.activation(out=ys_head, in_=ys[0][:, head], func=ACT.Copy)
         numerator(1)
         impact(1)
 
-        turned = [ps.tile([P, P], F32, name="turned%d" % b) for b in range(BLOCKS)]
+        turned = [ps.tile([P, P], F32, name="turned%d" % b, tag="bank%d" % b) for b in range(BLOCKS)]
         scaled = sb.tile([P, 3, HEAD], F32, name="scaled")
         for i in range(4):
             if i == 0:
@@ -219,11 +217,13 @@ def tile_picked_yimpct_cost_p_kernel(
                 nc.tensor.matmul(
                     turned[b][:], term[:, b * P : (b + 1) * P], ident[:], start=(i == 0), stop=(i == 3), is_transpose=True
                 )
+        ys_head = r[:, head]
+        nc.scalar.activation(out=ys_head, in_=ys[0][:, head], func=ACT.Copy)
         turned_sb = sb.tile([P, HEAD], F32, name="turned_sb")
-        move_head = ps.tile([P, HEAD], F32, name="move_head")
+        move_head = [ps.tile([P, PIECE], F32, name="move_head%d" % n) for n in range(2)]
         for b in range(BLOCKS):
             nc.scalar.copy(out=turned_sb[:, b * P : (b + 1) * P], in_=turned[b][:])
-            nc.tensor.transpose(move_head[:, b * P : (b + 1) * P], turned_sb[:, b * P : (b + 1) * P], ident[:])
+            nc.tensor.transpose(move_head[b // 2][:, b % 2 * P : (b % 2 + 1) * P], turned_sb[:, b * P : (b + 1) * P], ident[:])
 
         mid = (HEAD + S) // 2
         streams = (slice(HEAD, mid), slice(mid, S))
@@ -232,5 +232,7 @@ def tile_picked_yimpct_cost_p_kernel(
                 tap(i, cols)
         for cols in streams:
             cost(cols)
-        nc.vector.tensor_tensor(out=res[:, head], in0=move_head[:], in1=ys_head, op=ALU.mult)
-        nc.sync.dma_start(out=out[:, head], in_=res[:, head])
+        for n in range(2):
+            cols = slice(n * PIECE, (n + 1) * PIECE)
+            nc.vector.tensor_tensor(out=res[:, cols], in0=move_head[n][:], in1=ys_head[:, cols], op=ALU.mult)
+            nc.sync.dma_start(out=out[:, cols], in_=res[:, cols])

from contextlib import ExitStack

import concourse.mybir as mybir
from concourse.masks import make_identity

K, T, S, M = 512, 2048, 1024, 128
FLOPS = 2 * 2 * K * M * S

F32 = mybir.dt.float32
BF16 = mybir.dt.bfloat16
I32 = mybir.dt.int32
U32 = mybir.dt.uint32
U16 = mybir.dt.uint16
U8 = mybir.dt.uint8
FP8X4 = mybir.dt.float8_e4m3fn_x4
ALU = mybir.AluOpType
ACT = mybir.ActivationFunctionType

P = 128
PACK = 4
BANK = 512
PIECE = 256
PAD = 4
BLOCKS = 4
HEAD = BLOCKS * P
SOFT = 0.3
EXP_CAP = 2.0 ** 60
TINY = 1e-30


def tile_picked_yimpct_cost_p_kernel(
    tc, x_words, x_scales, w1, w2, ker1, ker2, ker3, offs, out
):
    nc = tc.nc
    with ExitStack() as ctx:
        sb = ctx.enter_context(tc.tile_pool(name="sb", bufs=1))
        ps = ctx.enter_context(tc.psum_pool(name="ps", bufs=1))

        offsets = sb.tile([P, S // 16], U16, name="offsets")
        nc.sync.dma_start(offsets[:], offs)

        scale_table = sb.tile([P, T], U8, name="scale_table", align_bytes=64)
        nc.vector.memset(scale_table[:].bitcast(I32), 0)
        w1_raw = sb.tile([P, PACK, M], F32, name="w1_raw")
        nc.sync.dma_start(out=w1_raw[:], in_=w1.rearrange("(p j) m -> p j m", j=PACK))
        for q, queue in enumerate((nc.sync, nc.scalar, nc.sync, nc.scalar)):
            queue.dma_start(
                out=scale_table[32 * q : 32 * q + 4, :].bitcast(I32),
                in_=x_scales[0, 4 * q : 4 * q + 4, :].bitcast(I32),
            )
        w2_raw = sb.tile([P, PACK, M], F32, name="w2_raw")
        nc.sync.dma_start(out=w2_raw[:], in_=w2.rearrange("(p j) m -> p j m", j=PACK))
        word_table = sb.tile([P, T], I32, name="word_table", align_bytes=64)
        nc.sync.dma_start(out=word_table[:], in_=x_words[0].rearrange("p c r -> p (c r)").bitcast(I32))

        kers = []
        for i, ker in enumerate((ker1, ker2, ker3)):
            col = sb.tile([P, 1], F32, name="ker%d" % (i + 1))
            nc.sync.dma_start(out=col[:], in_=ker)
            kers.append(col)

        imp = sb.tile([P, PAD + S], F32, name="imp")
        nc.vector.memset(imp[:, 1:PAD], 0.0)
        ident = sb.tile([P, P], F32, name="ident")
        nc.vector.memset(ident[:], 0.0)
        make_identity(nc, ident[:], nomemset=True)

        grouped = sb.tile([P, 2 * M * PACK], BF16, name="w_bf16", align_bytes=64)
        for i, raw in enumerate((w1_raw, w2_raw)):
            nc.scalar.activation(
                out=grouped[:, i * M * PACK : (i + 1) * M * PACK].rearrange("p (m j) -> p m j", j=PACK),
                in_=raw[:].rearrange("p j m -> p m j"),
                func=ACT.Copy,
            )

        x_codes = sb.tile([P, S], U32, name="x_codes", align_bytes=64)
        x_bytes = sb.tile([P, S], U8, name="x_bytes", align_bytes=64)
        nc.vector.tensor_copy(out=x_bytes[:], in_=scale_table[:].indirect(offsets[:]))

        w_codes = sb.tile([P, 2 * M], U32, name="w_codes", align_bytes=64)
        w_bytes = sb.tile([P, 2 * M], U8, name="w_bytes", align_bytes=64)
        nc.vector.quantize_mx(out=w_codes[:].bitcast(FP8X4), scales=w_bytes[:], in_=grouped[:])
        w1_q = (w_codes[:, 0:M], w_bytes[:, 0:M])
        w2_q = (w_codes[:, M : 2 * M], w_bytes[:, M : 2 * M])

        yv = [ps.tile([P, BANK], F32, name="yv%d" % h, tag="bank%d" % h) for h in range(2)]
        ys = [ps.tile([P, BANK], F32, name="ys%d" % h) for h in range(2)]
        e = sb.tile([P, S], F32, name="e")
        a = sb.tile([P, S], F32, name="a")

        def product(banks, weight, c0):
            cols = slice(c0, c0 + PIECE)
            target = banks[c0 // BANK][:, c0 % BANK : c0 % BANK + PIECE]
            nc.tensor.matmul_mx(
                out=target,
                lhsT=weight[0].bitcast(FP8X4),
                lhsT_scale=weight[1],
                rhs=x_codes[:, cols].bitcast(FP8X4),
                rhs_scale=x_bytes[:, cols],
                start=True,
                stop=True,
            )
            return target

        order = [0, 2 * PIECE, PIECE, 3 * PIECE]
        for n, c0 in enumerate(order):
            nc.vector.tensor_copy(
                out=x_codes[:, c0 : c0 + PIECE],
                in_=word_table[:].bitcast(U32).indirect(offsets[:, c0 // 16 : (c0 + PIECE) // 16]),
            )
            nc.scalar.activation(out=e[:, c0 : c0 + PIECE], in_=product(yv, w1_q, c0), func=ACT.Exp)
            if n < 2:
                nc.scalar.activation(out=a[:, c0 : c0 + PIECE], in_=product(ys, w2_q, c0), func=ACT.Abs)

        poly = sb.tile([P, S], F32, name="poly")

        def by_arrival(tile, late):
            return tile[:].rearrange("p (h l c) -> p l h c", h=2, l=2)[:, late]

        d = sb.tile([P, S], F32, name="d")

        def square(late):
            nc.vector.tensor_tensor(
                out=by_arrival(poly, late), in0=by_arrival(d, late), in1=by_arrival(d, late), op=ALU.mult
            )

        nc.vector.tensor_scalar(out=by_arrival(d, 0), in0=by_arrival(a, 0), scalar1=SOFT, scalar2=None, op0=ALU.add)
        square(0)
        ec = sb.tile([P, S], F32, name="ec")
        nc.gpsimd.tensor_scalar(out=ec[:], in0=e[:], scalar1=EXP_CAP, scalar2=0.0, op0=ALU.min, op1=ALU.max)

        neg_tile = sb.tile([P, BANK], F32, name="neg")
        neg = [neg_tile[:, 0:PIECE], neg_tile[:, PIECE:BANK]]
        late = [product(ys, w2_q, c0) for c0 in order[2:]]
        for n, signed in enumerate(late):
            nc.vector.tensor_scalar(out=neg[n], in0=signed, scalar1=-1.0, scalar2=SOFT, op0=ALU.mult, op1=ALU.add)
        for n, signed in enumerate(late):
            c0 = order[2 + n]
            nc.vector.scalar_tensor_tensor(
                out=d[:, c0 : c0 + PIECE], in0=signed, scalar=SOFT, in1=neg[n], op0=ALU.add, op1=ALU.max
            )
        square(1)

        halves = [slice(h * BANK, (h + 1) * BANK) for h in range(2)]
        lg_tile = sb.tile([P, S], F32, name="lg")
        lg = [lg_tile[:, 0:PIECE], lg_tile[:, PIECE:BANK], lg_tile[:, BANK:S]]
        for n, cols in enumerate((slice(0, PIECE), slice(PIECE, BANK), halves[1])):
            nc.scalar.activation(out=lg[n], in_=ec[:, cols], func=ACT.Ln, bias=1.0)

        sp = sb.tile([P, S], F32, name="sp")
        q = sb.tile([P, S], F32, name="q")
        num_tile = sb.tile([P, S], F32, name="num")
        r = sb.tile([P, S], F32, name="r")
        num = [num_tile[:, cols] for cols in halves]
        acc1 = sb.tile([P, S], F32, name="acc1")
        acc2 = sb.tile([P, S], F32, name="acc2")
        move = sb.tile([P, S], F32, name="move")
        res = sb.tile([P, S], F32, name="res")

        def stt(o, i0, s, i1, op0, op1):
            nc.vector.scalar_tensor_tensor(out=o, in0=i0, scalar=s, in1=i1, op0=op0, op1=op1)

        def volume(c0, n, log):
            bank = yv[c0 // BANK][:, c0 % BANK : c0 % BANK + n]
            stt(sp[:, c0 : c0 + n], bank, TINY, log, ALU.max, ALU.max)

        def radicand(h):
            cols = halves[h]
            engine = nc.vector if h == 0 else nc.gpsimd
            engine.tensor_tensor(out=q[:, cols], in0=poly[:, cols], in1=sp[:, cols], op=ALU.mult)
            nc.scalar.activation(out=r[:, cols], in_=q[:, cols], func=ACT.Abs_reciprocal_sqrt)

        def numerator(h):
            nc.vector.tensor_tensor(out=num[h], in0=ys[h][:], in1=sp[:, halves[h]], op=ALU.mult)

        def shifted(cols, by):
            return imp[:, PAD + cols.start - by : PAD + cols.stop - by]

        def impact(h):
            cols = halves[h]
            nc.vector.tensor_tensor(out=shifted(cols, 0), in0=num[h], in1=r[:, cols], op=ALU.mult)

        sums = [None, acc1, acc2, move]

        def tap(i, cols):
            before = shifted(cols, 0) if i == 1 else sums[i - 1][:, cols]
            stt(sums[i][:, cols], shifted(cols, i), kers[i - 1][:], before, ALU.mult, ALU.add)

        def cost(cols):
            cut = min(max(BANK, cols.start), cols.stop)
            for c0, c1 in ((cols.start, cut), (cut, cols.stop)):
                if c1 > c0:
                    signed = ys[c0 // BANK][:, c0 % BANK : c0 % BANK + c1 - c0]
                    nc.vector.tensor_tensor(out=res[:, c0:c1], in0=signed, in1=move[:, c0:c1], op=ALU.mult)
            nc.sync.dma_start(out=out[:, cols], in_=res[:, cols])

        volume(0, PIECE, lg[0])
        volume(PIECE, PIECE, lg[1])
        volume(BANK, BANK, lg[2])
        radicand(0)
        numerator(0)
        radicand(1)
        impact(0)
        head = slice(0, HEAD)
        numerator(1)
        impact(1)

        turned = [ps.tile([P, P], F32, name="turned%d" % b, tag="bank%d" % b) for b in range(BLOCKS)]
        scaled = sb.tile([P, 3, HEAD], F32, name="scaled")
        for i in range(4):
            if i == 0:
                term = shifted(head, 0)
            else:
                term = scaled[:, i - 1, :]
                nc.scalar.activation(out=term, in_=shifted(head, i), func=ACT.Copy, scale=kers[i - 1][:])
            for b in range(BLOCKS):
                nc.tensor.matmul(
                    turned[b][:], term[:, b * P : (b + 1) * P], ident[:], start=(i == 0), stop=(i == 3), is_transpose=True
                )
        ys_head = r[:, head]
        nc.scalar.activation(out=ys_head, in_=ys[0][:, head], func=ACT.Copy)
        turned_sb = sb.tile([P, HEAD], F32, name="turned_sb")
        move_head = [ps.tile([P, PIECE], F32, name="move_head%d" % n) for n in range(2)]
        for b in range(BLOCKS):
            nc.scalar.copy(out=turned_sb[:, b * P : (b + 1) * P], in_=turned[b][:])
            nc.tensor.transpose(move_head[b // 2][:, b % 2 * P : (b % 2 + 1) * P], turned_sb[:, b * P : (b + 1) * P], ident[:])

        mid = (HEAD + S) // 2
        streams = (slice(HEAD, mid), slice(mid, S))
        for i in (1, 2, 3):
            for cols in streams:
                tap(i, cols)
        for cols in streams:
            cost(cols)
        for n in range(2):
            cols = slice(n * PIECE, (n + 1) * PIECE)
            nc.vector.tensor_tensor(out=res[:, cols], in0=move_head[n][:], in1=ys_head[:, cols], op=ALU.mult)
            nc.sync.dma_start(out=out[:, cols], in_=res[:, cols])
